import numpy as np
import ml_dtypes


def mxq(x, axis, fmt="e4m3"):
    dtype, down = {"e4m3": (ml_dtypes.float8_e4m3fn, 7), "e5m2": (ml_dtypes.float8_e5m2, 14)}[fmt]
    v = np.moveaxis(np.asarray(x, np.float32).astype(ml_dtypes.bfloat16).astype(np.float64), axis, -1)
    blocks = v.reshape(v.shape[:-1] + (-1, 32))
    amax = np.abs(blocks).max(-1, keepdims=True)
    byte = np.maximum(np.where(amax > 0, np.frexp(amax)[1] - 1 + 127, 0) - down, 1)
    scale = np.exp2(byte - 127.0)
    codes = (blocks / scale).astype(np.float32).astype(dtype).astype(np.float64)
    return np.moveaxis((codes * scale).reshape(v.shape), -1, axis)


WIDE = False


def mx_kscale(k):
    if not WIDE:
        return np.ones(k)
    levels = np.array([10, -10, 5, -5, 0])
    if k % 512:
        return np.exp2(np.random.permutation(np.resize(levels, k // 32))).repeat(32)
    a = np.empty((k // 512, 16))
    for p in range(k // 512):
        a[p, :8] = np.random.permutation(np.resize(levels, 8))
        for g in range(8):
            far = levels[np.abs(levels - a[p, g]) >= 10]
            a[p, g + 8] = far[np.random.randint(len(far))]
    return np.exp2(a.ravel()).repeat(32)


def f64(x):
    return np.asarray(x).astype(np.float64)


def striped(idx):
    return np.tile(idx.reshape(-1, 16).T, (8, 1)).astype(np.uint16)


def unstriped(offs):
    return offs[:16].T.reshape(-1).astype(np.int64)


def pack_weight(w):
    k, n = w.shape
    w = f64(np.asarray(w, np.float32).astype(ml_dtypes.bfloat16)).reshape(k // 32, 32, n)
    amax = np.abs(w).max(1)
    byte = np.clip(np.where(amax > 0, np.frexp(amax)[1] - 1 + 127 - 7, 1), 1, 254)
    scaled = (w * np.exp2(127.0 - byte)[:, None, :]).reshape(k, n).astype(np.float32)
    words = np.ascontiguousarray(scaled.reshape(k // 512, 128, 4, n).transpose(0, 1, 3, 2)).astype(ml_dtypes.float8_e4m3fn).view(np.uint8)
    return words, np.ascontiguousarray(byte.astype(np.uint8).reshape(k // 512, 16, n))


def unpack_weight(words, scales):
    g, p, n, _ = words.shape
    vals = np.ascontiguousarray(words).view(ml_dtypes.float8_e4m3fn).astype(np.float64) * np.repeat(np.exp2(scales.astype(np.float64) - 127.0), 8, axis=1)[..., None]
    return vals.transpose(0, 1, 3, 2).reshape(g * 512, n)


K, T, D, S, V, N = 512, 2048, 8, 1024, 128, 512


def setup_inputs():
    n = np.random.standard_normal
    s = mx_kscale(K)[:, None]
    words, scales = pack_weight(n((K, N)) / np.sqrt(K) / s)
    return {
        "xT": (n((K, T)) * s).astype(np.float32),
        "w_words": words,
        "w_scales": scales,
        "b": (0.3 * n((N, 1))).astype(np.float32),
        "offs": striped(np.random.permutation(T)[:S]),
    }


def reference(xT, w_words, w_scales, b, offs):
    w = unpack_weight(w_words, w_scales)
    idx = unstriped(offs)
    xq = mxq(f64(xT)[:, idx], 0, "e4m3")
    y = w.T @ xq
    y = y + f64(b)
    return y.reshape(N, V, D).max(axis=2)

@@ -1,0 +1,182 @@
+from contextlib import ExitStack
+
+import concourse.mybir as mybir
+
+K, T, S, D, V, M = 512, 2048, 1024, 8, 128, 512
+FLOPS = 2 * K * S * M
+
+F32 = mybir.dt.float32
+BF16 = mybir.dt.bfloat16
+I32 = mybir.dt.int32
+U32 = mybir.dt.uint32
+U16 = mybir.dt.uint16
+U8 = mybir.dt.uint8
+FP8X4 = mybir.dt.float8_e4m3fn_x4
+IDENT = mybir.ActivationFunctionType.Identity
+COPY = mybir.ActivationFunctionType.Copy
+MAX = mybir.AluOpType.max
+AXIS_X = mybir.AxisListType.X
+
+P = 128
+NS = 256
+SLICES = S // NS
+MT = M // P
+CH = 4
+CW = T // CH
+TH = T // 2
+HALF = S // 2
+VH = HALF // D
+
+
+def tile_picked_pool_lin_bias_sub_e_kernel(tc, xT, w_words, w_scales, b, offs, out):
+    nc = tc.nc
+    with ExitStack() as ctx:
+        keep = ctx.enter_context(tc.tile_pool(name="keep", bufs=1))
+        psum = ctx.enter_context(tc.psum_pool(name="psum", bufs=1))
+
+        offsets = keep.tile([P, S // 16], U16, name="offsets")
+        nc.sync.dma_start(offsets[:], offs)
+
+        planes = xT.rearrange("(p t) n -> p t n", t=4)
+        raw01 = []
+        for c in range(CH):
+            r = keep.tile([P, 2, CW], F32, name=f"raw01_{c}")
+            nc.sync.dma_start(r[:], planes[:, 0:2, c * CW : (c + 1) * CW])
+            raw01.append(r)
+        raw = {}
+        for t in (2, 3):
+            r = keep.tile([P, T], F32, name=f"raw{t}")
+            for c in range(2):
+                nc.sync.dma_start(r[:, c * TH : (c + 1) * TH], planes[:, t, c * TH : (c + 1) * TH])
+            raw[t] = r
+
+        words = keep.tile([P, M], I32, name="words", align_bytes=64)
+        nc.sync.dma_start(words[:], w_words[0].rearrange("p m r -> p (m r)").bitcast(I32))
+
+        w_sc = keep.tile([P, M], U8, name="w_sc", align_bytes=64)
+        nc.vector.memset(w_sc[:].bitcast(I32), 0)
+        for q in range(4):
+            nc.scalar.dma_start(w_sc[32 * q : 32 * q + 4, :].bitcast(I32), w_scales[0, 4 * q : 4 * q + 4, :].bitcast(I32))
+        bias = keep.tile([P, MT], F32, name="bias")
+        nc.gpsimd.dma_start(bias[:], b.rearrange("(i p) o -> p (i o)", p=P))
+
+        warm = keep.tile([P, 8], F32, name="warm")
+        nc.gpsimd.memset(warm[:], 0.0)
+        nc.scalar.activation(warm[:, 0:2], warm[:, 4:6], IDENT)
+
+        acc = [[psum.tile([P, HALF], F32, name=f"acc{h}_{i}") for i in range(MT)] for h in range(2)]
+
+        pairs = keep.tile([P, T, 2], BF16, name="pairs")
+        table = {t: keep.tile([P, T], BF16, name=f"table{t}") for t in (2, 3)}
+        grouped = [keep.tile([P, NS, 4], BF16, name=f"grouped{s}", align_bytes=64) for s in range(SLICES)]
+        codes = [keep.tile([P, NS], U32, name=f"codes{s}", align_bytes=64) for s in range(SLICES)]
+        scales = [keep.tile([P, NS], U8, name=f"scales{s}", align_bytes=64) for s in range(SLICES)]
+
+        def lst(s):
+            return offsets[:, s * NS // 16 : (s + 1) * NS // 16]
+
+        def cast_pairs(eng, c, a, n):
+            o = pairs[:, c * CW + a : c * CW + a + n, :]
+            i = raw01[c][:, :, a : a + n].rearrange("p t n -> p n t")
+            if eng == "V":
+                nc.vector.tensor_copy(o, i)
+            else:
+                nc.scalar.copy(o, i)
+
+        def cast_plane(eng, t, c):
+            o = table[t][:, c * TH : (c + 1) * TH]
+            i = raw[t][:, c * TH : (c + 1) * TH]
+            if eng == "V":
+                nc.vector.tensor_copy(o, i)
+            else:
+                nc.scalar.copy(o, i)
+
+        def gather_pairs(s):
+            dst = grouped[s][:].rearrange("p n t -> p (n t)").bitcast(U32).rearrange("p (n u) -> p n u", u=2)[:, :, 0]
+            win = pairs[:].rearrange("p n t -> p (n t)").bitcast(U32)
+            nc.vector.tensor_copy(dst, win.indirect(lst(s)))
+
+        def gather_vector(s, t):
+            nc.vector.tensor_copy(grouped[s][:, :, t], raw[t][:].indirect(lst(s)))
+
+        def gather_scalar(s, t):
+            nc.scalar.activation(grouped[s][:, :, t], table[t][:].indirect(lst(s)), COPY)
+
+        def quantise(s):
+            nc.vector.quantize_mx(
+                out=codes[s][:].bitcast(FP8X4),
+                scales=scales[s][:],
+                in_=grouped[s][:].rearrange("p n t -> p (n t)"),
+            )
+
+        def multiply(s, i):
+            h, c = divmod(s, 2)
+            nc.tensor.matmul_mx(
+                out=acc[h][i][:, c * NS : (c + 1) * NS],
+                lhsT=words[:, i * P : (i + 1) * P].bitcast(FP8X4),
+                lhsT_scale=w_sc[:, i * P : (i + 1) * P],
+                rhs=codes[s][:].bitcast(FP8X4),
+                rhs_scale=scales[s][:],
+                start=True,
+                stop=True,
+            )
+
+        pooled = keep.tile([P, MT, V], F32, name="pooled")
+        result = keep.tile([P, MT, V], F32, name="result")
+        biased = keep.tile([P, HALF], F32, name="biased")
+        late = keep.tile([P, VH], F32, name="late")
+        out_view = out.rearrange("(i p) v -> p i v", p=P)
+
+        def pool_max(h, i):
+            nc.vector.tensor_reduce(
+                out=pooled[:, i, h * VH : (h + 1) * VH],
+                in_=acc[h][i][:].rearrange("p (v d) -> p v d", d=D),
+                axis=AXIS_X,
+                op=MAX,
+            )
+
+        def add_bias(h, i):
+            nc.scalar.activation(
+                result[:, i, h * VH : (h + 1) * VH], pooled[:, i, h * VH : (h + 1) * VH], IDENT, bias=bias[:, i : i + 1]
+            )
+
+        cast_pairs("S", 0, 0, CW)
+        cast_pairs("V", 1, 0, CW)
+        cast_pairs("V", 2, 0, CW)
+        cast_pairs("V", 3, 0, CW)
+        for s in range(SLICES):
+            gather_pairs(s)
+        cast_plane("S", 2, 0)
+        cast_plane("S", 2, 1)
+        cast_plane("S", 3, 0)
+        for s in (2, 3):
+            gather_scalar(s, 2)
+        for s in (0, 1):
+            gather_vector(s, 2)
+        cast_plane("V", 3, 1)
+        for s in (2, 3):
+            gather_scalar(s, 3)
+        for s in (0, 1):
+            gather_vector(s, 3)
+        for s in range(2):
+            quantise(s)
+        for i in range(MT):
+            multiply(0, i)
+            multiply(1, i)
+        for s in (2, 3):
+            quantise(s)
+        for i in range(MT):
+            multiply(2, i)
+            multiply(3, i)
+        for i in range(MT):
+            pool_max(0, i)
+            add_bias(0, i)
+        nc.sync.dma_start(out_view[:, :, 0:VH], result[:, :, 0:VH])
+        last = MT - 1
+        nc.scalar.activation(biased[:], acc[1][last][:], IDENT, bias=bias[:, last:MT])
+        for i in range(last):
+            pool_max(1, i)
+            add_bias(1, i)
+            nc.sync.dma_start(out_view[:, i, VH:V], result[:, i, VH:V])
+        nc.vector.tensor_reduce(out=late[:], in_=biased[:].rearrange("p (v d) -> p v d", d=D), axis=AXIS_X, op=MAX)
+        nc.sync.dma_start(out_view[:, last, VH:V], late[:])

@@ -14,6 +14,8 @@ U8 = mybir.dt.uint8
 FP8X4 = mybir.dt.float8_e4m3fn_x4
 IDENT = mybir.ActivationFunctionType.Identity
 COPY = mybir.ActivationFunctionType.Copy
+MULT = mybir.AluOpType.mult
+ADD = mybir.AluOpType.add
 MAX = mybir.AluOpType.max
 AXIS_X = mybir.AxisListType.X
 
@@ -21,8 +23,6 @@ P = 128
 NS = 256
 SLICES = S // NS
 MT = M // P
-CH = 4
-CW = T // CH
 TH = T // 2
 HALF = S // 2
 VH = HALF // D
@@ -38,17 +38,12 @@ def tile_picked_pool_lin_bias_sub_e_kernel(tc, xT, w_words, w_scales, b, offs, o
         nc.sync.dma_start(offsets[:], offs)
 
         planes = xT.rearrange("(p t) n -> p t n", t=4)
-        raw01 = []
-        for c in range(CH):
-            r = keep.tile([P, 2, CW], F32, name=f"raw01_{c}")
-            nc.sync.dma_start(r[:], planes[:, 0:2, c * CW : (c + 1) * CW])
-            raw01.append(r)
-        raw = {}
-        for t in (2, 3):
+        raw = []
+        for t, cuts in enumerate(((0, T), (0, T), (0, TH, T), (0, TH, 3 * TH // 2, T))):
             r = keep.tile([P, T], F32, name=f"raw{t}")
-            for c in range(2):
-                nc.sync.dma_start(r[:, c * TH : (c + 1) * TH], planes[:, t, c * TH : (c + 1) * TH])
-            raw[t] = r
+            for lo, hi in zip(cuts, cuts[1:]):
+                nc.sync.dma_start(r[:, lo:hi], planes[:, t, lo:hi])
+            raw.append(r)
 
         words = keep.tile([P, M], I32, name="words", align_bytes=64)
         nc.sync.dma_start(words[:], w_words[0].rearrange("p m r -> p (m r)").bitcast(I32))
@@ -66,7 +61,7 @@ def tile_picked_pool_lin_bias_sub_e_kernel(tc, xT, w_words, w_scales, b, offs, o
 
         acc = [[psum.tile([P, HALF], F32, name=f"acc{h}_{i}") for i in range(MT)] for h in range(2)]
 
-        pairs = keep.tile([P, T, 2], BF16, name="pairs")
+        low = keep.tile([P, 2, S], F32, name="low")
         table = {t: keep.tile([P, T], BF16, name=f"table{t}") for t in (2, 3)}
         grouped = [keep.tile([P, NS, 4], BF16, name=f"grouped{s}", align_bytes=64) for s in range(SLICES)]
         codes = [keep.tile([P, NS], U32, name=f"codes{s}", align_bytes=64) for s in range(SLICES)]
@@ -75,26 +70,28 @@ def tile_picked_pool_lin_bias_sub_e_kernel(tc, xT, w_words, w_scales, b, offs, o
         def lst(s):
             return offsets[:, s * NS // 16 : (s + 1) * NS // 16]
 
-        def cast_pairs(eng, c, a, n):
-            o = pairs[:, c * CW + a : c * CW + a + n, :]
-            i = raw01[c][:, :, a : a + n].rearrange("p t n -> p n t")
+        def cast_plane(eng, t, lo, hi):
+            o = table[t][:, lo:hi]
+            i = raw[t][:, lo:hi]
             if eng == "V":
                 nc.vector.tensor_copy(o, i)
             else:
                 nc.scalar.copy(o, i)
 
-        def cast_plane(eng, t, c):
-            o = table[t][:, c * TH : (c + 1) * TH]
-            i = raw[t][:, c * TH : (c + 1) * TH]
-            if eng == "V":
-                nc.vector.tensor_copy(o, i)
-            else:
-                nc.scalar.copy(o, i)
+        def gather_low(t, a, n):
+            lst2 = offsets[:] if n == S else offsets[:, a // 16 : (a + n) // 16]
+            nc.vector.tensor_copy(low[:, t, a : a + n], raw[t][:].indirect(lst2))
 
-        def gather_pairs(s):
-            dst = grouped[s][:].rearrange("p n t -> p (n t)").bitcast(U32).rearrange("p (n u) -> p n u", u=2)[:, :, 0]
-            win = pairs[:].rearrange("p n t -> p (n t)").bitcast(U32)
-            nc.vector.tensor_copy(dst, win.indirect(lst(s)))
+        def interleave(s):
+            sl = slice(s * NS, (s + 1) * NS)
+            if s < 2:
+                nc.gpsimd.tensor_scalar(
+                    grouped[s][:].rearrange("p n (r t) -> p n r t", t=2),
+                    low[:, :, sl].rearrange("p t n -> p n t").unsqueeze(2).broadcast_to([P, NS, 2, 2]),
+                    1.0, 0.0, MULT, ADD,
+                )
+            else:
+                nc.gpsimd.tensor_scalar(grouped[s][:, :, 0:2], low[:, :, sl].rearrange("p t n -> p n t"), 1.0, 0.0, MULT, ADD)
 
         def gather_vector(s, t):
             nc.vector.tensor_copy(grouped[s][:, :, t], raw[t][:].indirect(lst(s)))
@@ -140,20 +137,19 @@ def tile_picked_pool_lin_bias_sub_e_kernel(tc, xT, w_words, w_scales, b, offs, o
                 result[:, i, h * VH : (h + 1) * VH], pooled[:, i, h * VH : (h + 1) * VH], IDENT, bias=bias[:, i : i + 1]
             )
 
-        cast_pairs("S", 0, 0, CW)
-        cast_pairs("V", 1, 0, CW)
-        cast_pairs("V", 2, 0, CW)
-        cast_pairs("V", 3, 0, CW)
+        gather_low(0, 0, S)
         for s in range(SLICES):
-            gather_pairs(s)
-        cast_plane("S", 2, 0)
-        cast_plane("S", 2, 1)
-        cast_plane("S", 3, 0)
+            gather_low(1, s * NS, NS)
+            interleave(s)
+        cast_plane("S", 2, 0, TH)
+        cast_plane("S", 2, TH, T)
         for s in (2, 3):
             gather_scalar(s, 2)
         for s in (0, 1):
             gather_vector(s, 2)
-        cast_plane("V", 3, 1)
+        cast_plane("V", 3, 0, TH)
+        cast_plane("V", 3, TH, 3 * TH // 2)
+        cast_plane("V", 3, 3 * TH // 2, T)
         for s in (2, 3):
             gather_scalar(s, 3)
         for s in (0, 1):

@@ -53,7 +53,7 @@ def tile_picked_pool_lin_bias_sub_e_kernel(tc, xT, w_words, w_scales, b, offs, o
         for q in range(4):
             nc.scalar.dma_start(w_sc[32 * q : 32 * q + 4, :].bitcast(I32), w_scales[0, 4 * q : 4 * q + 4, :].bitcast(I32))
         bias = keep.tile([P, MT], F32, name="bias")
-        nc.gpsimd.dma_start(bias[:], b.rearrange("(i p) o -> p (i o)", p=P))
+        nc.sync.dma_start(bias[:], b.rearrange("(i p) o -> p (i o)", p=P))
 
         warm = keep.tile([P, 8], F32, name="warm")
         nc.gpsimd.memset(warm[:], 0.0)
@@ -138,8 +138,11 @@ def tile_picked_pool_lin_bias_sub_e_kernel(tc, xT, w_words, w_scales, b, offs, o
             )
 
         gather_low(0, 0, S)
-        for s in range(SLICES):
+        for s in range(2):
             gather_low(1, s * NS, NS)
+            interleave(s)
+        gather_low(1, HALF, HALF)
+        for s in (2, 3):
             interleave(s)
         cast_plane("S", 2, 0, TH)
         cast_plane("S", 2, TH, T)
@@ -149,7 +152,7 @@ def tile_picked_pool_lin_bias_sub_e_kernel(tc, xT, w_words, w_scales, b, offs, o
             gather_vector(s, 2)
         cast_plane("V", 3, 0, TH)
         cast_plane("V", 3, TH, 3 * TH // 2)
-        cast_plane("V", 3, 3 * TH // 2, T)
+        cast_plane("S", 3, 3 * TH // 2, T)
         for s in (2, 3):
             gather_scalar(s, 3)
         for s in (0, 1):

from contextlib import ExitStack

import concourse.mybir as mybir

K, T, S, D, V, M = 512, 2048, 1024, 8, 128, 512
FLOPS = 2 * K * S * M

F32 = mybir.dt.float32
BF16 = mybir.dt.bfloat16
I32 = mybir.dt.int32
U32 = mybir.dt.uint32
U16 = mybir.dt.uint16
U8 = mybir.dt.uint8
FP8X4 = mybir.dt.float8_e4m3fn_x4
IDENT = mybir.ActivationFunctionType.Identity
COPY = mybir.ActivationFunctionType.Copy
MULT = mybir.AluOpType.mult
ADD = mybir.AluOpType.add
MAX = mybir.AluOpType.max
AXIS_X = mybir.AxisListType.X

P = 128
NS = 256
SLICES = S // NS
MT = M // P
TH = T // 2
HALF = S // 2
VH = HALF // D


def tile_picked_pool_lin_bias_sub_e_kernel(tc, xT, w_words, w_scales, b, offs, out):
    nc = tc.nc
    with ExitStack() as ctx:
        keep = ctx.enter_context(tc.tile_pool(name="keep", bufs=1))
        psum = ctx.enter_context(tc.psum_pool(name="psum", bufs=1))

        offsets = keep.tile([P, S // 16], U16, name="offsets")
        nc.sync.dma_start(offsets[:], offs)

        planes = xT.rearrange("(p t) n -> p t n", t=4)
        raw = []
        for t, cuts in enumerate(((0, T), (0, T), (0, TH, T), (0, TH, 3 * TH // 2, T))):
            r = keep.tile([P, T], F32, name=f"raw{t}")
            for lo, hi in zip(cuts, cuts[1:]):
                nc.sync.dma_start(r[:, lo:hi], planes[:, t, lo:hi])
            raw.append(r)

        words = keep.tile([P, M], I32, name="words", align_bytes=64)
        nc.sync.dma_start(words[:], w_words[0].rearrange("p m r -> p (m r)").bitcast(I32))

        w_sc = keep.tile([P, M], U8, name="w_sc", align_bytes=64)
        nc.vector.memset(w_sc[:].bitcast(I32), 0)
        for q in range(4):
            nc.scalar.dma_start(w_sc[32 * q : 32 * q + 4, :].bitcast(I32), w_scales[0, 4 * q : 4 * q + 4, :].bitcast(I32))
        bias = keep.tile([P, MT], F32, name="bias")
        nc.sync.dma_start(bias[:], b.rearrange("(i p) o -> p (i o)", p=P))

        warm = keep.tile([P, 8], F32, name="warm")
        nc.gpsimd.memset(warm[:], 0.0)
        nc.scalar.activation(warm[:, 0:2], warm[:, 4:6], IDENT)

        acc = [[psum.tile([P, HALF], F32, name=f"acc{h}_{i}") for i in range(MT)] for h in range(2)]

        low = keep.tile([P, 2, S], F32, name="low")
        table = {t: keep.tile([P, T], BF16, name=f"table{t}") for t in (2, 3)}
        grouped = [keep.tile([P, NS, 4], BF16, name=f"grouped{s}", align_bytes=64) for s in range(SLICES)]
        codes = [keep.tile([P, NS], U32, name=f"codes{s}", align_bytes=64) for s in range(SLICES)]
        scales = [keep.tile([P, NS], U8, name=f"scales{s}", align_bytes=64) for s in range(SLICES)]

        def lst(s):
            return offsets[:, s * NS // 16 : (s + 1) * NS // 16]

        def cast_plane(eng, t, lo, hi):
            o = table[t][:, lo:hi]
            i = raw[t][:, lo:hi]
            if eng == "V":
                nc.vector.tensor_copy(o, i)
            else:
                nc.scalar.copy(o, i)

        def gather_low(t, a, n):
            lst2 = offsets[:] if n == S else offsets[:, a // 16 : (a + n) // 16]
            nc.vector.tensor_copy(low[:, t, a : a + n], raw[t][:].indirect(lst2))

        def interleave(s):
            sl = slice(s * NS, (s + 1) * NS)
            if s < 2:
                nc.gpsimd.tensor_scalar(
                    grouped[s][:].rearrange("p n (r t) -> p n r t", t=2),
                    low[:, :, sl].rearrange("p t n -> p n t").unsqueeze(2).broadcast_to([P, NS, 2, 2]),
                    1.0, 0.0, MULT, ADD,
                )
            else:
                nc.gpsimd.tensor_scalar(grouped[s][:, :, 0:2], low[:, :, sl].rearrange("p t n -> p n t"), 1.0, 0.0, MULT, ADD)

        def gather_vector(s, t):
            nc.vector.tensor_copy(grouped[s][:, :, t], raw[t][:].indirect(lst(s)))

        def gather_scalar(s, t):
            nc.scalar.activation(grouped[s][:, :, t], table[t][:].indirect(lst(s)), COPY)

        def quantise(s):
            nc.vector.quantize_mx(
                out=codes[s][:].bitcast(FP8X4),
                scales=scales[s][:],
                in_=grouped[s][:].rearrange("p n t -> p (n t)"),
            )

        def multiply(s, i):
            h, c = divmod(s, 2)
            nc.tensor.matmul_mx(
                out=acc[h][i][:, c * NS : (c + 1) * NS],
                lhsT=words[:, i * P : (i + 1) * P].bitcast(FP8X4),
                lhsT_scale=w_sc[:, i * P : (i + 1) * P],
                rhs=codes[s][:].bitcast(FP8X4),
                rhs_scale=scales[s][:],
                start=True,
                stop=True,
            )

        pooled = keep.tile([P, MT, V], F32, name="pooled")
        result = keep.tile([P, MT, V], F32, name="result")
        biased = keep.tile([P, HALF], F32, name="biased")
        late = keep.tile([P, VH], F32, name="late")
        out_view = out.rearrange("(i p) v -> p i v", p=P)

        def pool_max(h, i):
            nc.vector.tensor_reduce(
                out=pooled[:, i, h * VH : (h + 1) * VH],
                in_=acc[h][i][:].rearrange("p (v d) -> p v d", d=D),
                axis=AXIS_X,
                op=MAX,
            )

        def add_bias(h, i):
            nc.scalar.activation(
                result[:, i, h * VH : (h + 1) * VH], pooled[:, i, h * VH : (h + 1) * VH], IDENT, bias=bias[:, i : i + 1]
            )

        gather_low(0, 0, S)
        for s in range(2):
            gather_low(1, s * NS, NS)
            interleave(s)
        gather_low(1, HALF, HALF)
        for s in (2, 3):
            interleave(s)
        cast_plane("S", 2, 0, TH)
        cast_plane("S", 2, TH, T)
        for s in (2, 3):
            gather_scalar(s, 2)
        for s in (0, 1):
            gather_vector(s, 2)
        cast_plane("V", 3, 0, TH)
        cast_plane("V", 3, TH, 3 * TH // 2)
        cast_plane("S", 3, 3 * TH // 2, T)
        for s in (2, 3):
            gather_scalar(s, 3)
        for s in (0, 1):
            gather_vector(s, 3)
        for s in range(2):
            quantise(s)
        for i in range(MT):
            multiply(0, i)
            multiply(1, i)
        for s in (2, 3):
            quantise(s)
        for i in range(MT):
            multiply(2, i)
            multiply(3, i)
        for i in range(MT):
            pool_max(0, i)
            add_bias(0, i)
        nc.sync.dma_start(out_view[:, :, 0:VH], result[:, :, 0:VH])
        last = MT - 1
        nc.scalar.activation(biased[:], acc[1][last][:], IDENT, bias=bias[:, last:MT])
        for i in range(last):
            pool_max(1, i)
            add_bias(1, i)
            nc.sync.dma_start(out_view[:, i, VH:V], result[:, i, VH:V])
        nc.vector.tensor_reduce(out=late[:], in_=biased[:].rearrange("p (v d) -> p v d", d=D), axis=AXIS_X, op=MAX)
        nc.sync.dma_start(out_view[:, last, VH:V], late[:])
